import numpy as np
import ml_dtypes


def mxq(x, axis, fmt="e4m3"):
    dtype, down = {"e4m3": (ml_dtypes.float8_e4m3fn, 7), "e5m2": (ml_dtypes.float8_e5m2, 14)}[fmt]
    v = np.moveaxis(np.asarray(x, np.float32).astype(ml_dtypes.bfloat16).astype(np.float64), axis, -1)
    blocks = v.reshape(v.shape[:-1] + (-1, 32))
    amax = np.abs(blocks).max(-1, keepdims=True)
    byte = np.maximum(np.where(amax > 0, np.frexp(amax)[1] - 1 + 127, 0) - down, 1)
    scale = np.exp2(byte - 127.0)
    codes = (blocks / scale).astype(np.float32).astype(dtype).astype(np.float64)
    return np.moveaxis((codes * scale).reshape(v.shape), -1, axis)


WIDE = False


def mx_kscale(k):
    if not WIDE:
        return np.ones(k)
    levels = np.array([10, -10, 5, -5, 0])
    if k % 512:
        return np.exp2(np.random.permutation(np.resize(levels, k // 32))).repeat(32)
    a = np.empty((k // 512, 16))
    for p in range(k // 512):
        a[p, :8] = np.random.permutation(np.resize(levels, 8))
        for g in range(8):
            far = levels[np.abs(levels - a[p, g]) >= 10]
            a[p, g + 8] = far[np.random.randint(len(far))]
    return np.exp2(a.ravel()).repeat(32)


BF16 = ml_dtypes.bfloat16


def bf(x):
    return np.asarray(x, np.float32).astype(BF16)


def f64(x):
    return np.asarray(x).astype(np.float64)


E2M1 = np.array([0.0, 0.5, 1.0, 1.5, 2.0, 3.0, 4.0, 6.0, -0.0, -0.5, -1.0, -1.5, -2.0, -3.0, -4.0, -6.0])


def pack_weight(w, fmt):
    k, n = w.shape
    w = f64(bf(w)).reshape(k // 32, 32, n)
    amax = np.abs(w).max(1)
    if fmt == "e4m3":
        byte = np.frexp(amax)[1] - 1 + 127 - 7
    else:
        mant, ex = np.frexp(amax / 6.0)
        byte = np.where(mant > 0.5, ex, ex - 1) + 127
    byte = np.clip(np.where(amax > 0, byte, 1), 1, 254)
    scaled = (w * np.exp2(127.0 - byte)[:, None, :]).reshape(k, n).astype(np.float32)
    by_word = np.ascontiguousarray(scaled.reshape(k // 512, 128, 4, n).transpose(0, 1, 3, 2))
    if fmt == "e4m3":
        words = by_word.astype(ml_dtypes.float8_e4m3fn).view(np.uint8)
    else:
        c = by_word.astype(ml_dtypes.float4_e2m1fn).view(np.uint8) & 0xF
        words = c[..., 0::2] | (c[..., 1::2] << 4)
    return np.ascontiguousarray(words), np.ascontiguousarray(byte.astype(np.uint8).reshape(k // 512, 16, n))


def unpack_weight(words, scales, fmt):
    g, p, n, _ = words.shape
    if fmt == "e4m3":
        vals = np.ascontiguousarray(words).view(ml_dtypes.float8_e4m3fn).astype(np.float64)
    else:
        nib = np.empty((g, p, n, 4), np.uint8)
        nib[..., 0::2] = words & 0xF
        nib[..., 1::2] = words >> 4
        vals = E2M1[nib]
    vals = vals * np.repeat(np.exp2(scales.astype(np.float64) - 127.0), 8, axis=1)[..., None]
    return vals.transpose(0, 1, 3, 2).reshape(g * 512, n)
def pack4(w):
    words, scales = pack_weight(w, "e2m1")
    return words.reshape(words.shape[0], 128, -1), scales


def unpack4(words, scales):
    return unpack_weight(words.reshape(words.shape[0], 128, -1, 2), scales, "e2m1")


G, C, N = 2048, 512, 2048


def draw0():
    s, t = mx_kscale(C), mx_kscale(G)
    sig = np.exp(1.2 * np.random.standard_normal((G, C)) - 0.72)
    content = np.exp(0.4 * np.random.standard_normal(N))
    depth = np.exp(0.4 * np.random.standard_normal(N))
    h = np.exp(np.random.standard_normal((C, N)) - 0.5) * content
    bulk = np.exp(np.random.standard_normal((G, N)) - 0.5) * depth
    norm_words, norm_scales = pack4(sig / np.sum(sig, axis=0) / t[:, None] / s)
    return {"sig": bf(sig / C / s),
            "h": bf(h * s[:, None]),
            "ambient": bf(0.3 * np.exp(0.5 * np.random.standard_normal(G))),
            "bulk": bf(bulk * t[:, None]),
            "norm_words": norm_words,
            "norm_scales": norm_scales}


def core(sig, h, ambient, bulk, norm_words, norm_scales):
    hf = f64(h)
    r = mxq(f64(sig), 1, "e4m3") @ mxq(hf, 0, "e4m3")
    ratio = f64(bulk) / (r + f64(ambient)[:, None])
    w = unpack4(norm_words, norm_scales)
    u = w.T @ mxq(ratio, 0, "e4m3")
    return hf * u


def e4m3fn_bytes(y):
    return np.clip(np.asarray(y, np.float64), -448.0, 448.0).astype(np.float32).astype(ml_dtypes.float8_e4m3fn).view(np.uint8)


def e4m3fn_values(b):
    return np.asarray(b, np.uint8).view(ml_dtypes.float8_e4m3fn).astype(np.float64)


def setup_inputs():
    d = draw0()
    x0 = np.asarray(d['sig']).astype(np.float64)
    s = (np.max(np.abs(x0), axis=(0,), keepdims=True) / 448.0).astype(np.float32)
    out = {}
    for k, v in d.items():
        if k == 'sig':
            out['sig_bytes'] = e4m3fn_bytes(x0 / s.astype(np.float64))
            out['sig_scale'] = s
        else:
            out[k] = v
    return out


def reference(sig_bytes, sig_scale, h, ambient, bulk, norm_words, norm_scales):
    return core(e4m3fn_values(sig_bytes) * sig_scale.astype(np.float64), h, ambient, bulk, norm_words, norm_scales)

@@ -1,0 +1,265 @@
+from contextlib import ExitStack
+
+import concourse.mybir as mybir
+from concourse.masks import make_identity
+
+GENES, TYPES, SAMPLES = 2048, 512, 2048
+FLOPS = 2 * 2 * GENES * TYPES * SAMPLES
+
+F32 = mybir.dt.float32
+BF16 = mybir.dt.bfloat16
+U32 = mybir.dt.uint32
+I32 = mybir.dt.int32
+U8 = mybir.dt.uint8
+F8 = mybir.dt.float8_e4m3fn
+E4 = mybir.dt.float8_e4m3fn_x4
+E2 = mybir.dt.float4_e2m1fn_x4
+ACT = mybir.ActivationFunctionType
+MULT = mybir.AluOpType.mult
+
+P = 128
+NB = 512
+GROUPS = GENES // 512
+CHUNKS = SAMPLES // NB
+UNITS = GROUPS * CHUNKS
+V_SQUARES = {(5, 1), (9, 1), (13, 1)}
+
+
+def tile_deconvolution_multiplicative_update_s13_kernel(tc, sig_bytes, sig_scale, h, ambient, bulk, norm_words, norm_scales, out):
+    nc = tc.nc
+    with ExitStack() as ctx:
+        keep = ctx.enter_context(tc.tile_pool(name="keep", bufs=1))
+        two = ctx.enter_context(tc.tile_pool(name="two", bufs=2))
+        three = ctx.enter_context(tc.tile_pool(name="three", bufs=3))
+        psum = ctx.enter_context(tc.psum_pool(name="psum", bufs=1))
+        ctx.enter_context(tc.manual_schedule())
+
+        ident = keep.tile([P, P], F32, name="ident")
+        ones = keep.tile([P, 1], F32, name="ones")
+        junk = keep.tile([P, 1], F32, name="junk")
+        scale = keep.tile([P, 1, 2, 2], F32, name="scale")
+        amb = keep.tile([P, GROUPS, 4], BF16, name="amb")
+        words = keep.tile([P, GROUPS, 1024], U8, name="words", align_bytes=64)
+        wsc = keep.tile([P, GROUPS, TYPES], U8, name="wsc", align_bytes=64)
+        codes_in = [keep.tile([P, 2048], U8, name=f"sigraw{g}", align_bytes=64) for g in range(GROUPS)]
+        h_first = keep.tile([P, 4, NB], BF16, name="h_first", align_bytes=64)
+        h_rest = keep.tile([P, 4, SAMPLES - NB], BF16, name="h_rest", align_bytes=64)
+        h_out = keep.tile([P, 4, SAMPLES], BF16, name="h_out", align_bytes=64)
+        b_first = [keep.tile([P, 4, NB], BF16, name=f"b_first{g}", align_bytes=64) for g in range(GROUPS)]
+        b_rest = [keep.tile([P, 4, SAMPLES - NB], BF16, name=f"b_rest{g}", align_bytes=64) for g in range(GROUPS)]
+        sig_c = [keep.tile([P, 512], U32, name=f"sig_c{g}", align_bytes=64) for g in range(GROUPS)]
+        sig_s = [keep.tile([P, 512], U8, name=f"sig_s{g}", align_bytes=64) for g in range(GROUPS)]
+        h_c = [keep.tile([P, NB], U32, name=f"h_c{j}", align_bytes=64) for j in range(CHUNKS)]
+        h_s = [keep.tile([P, NB], U8, name=f"h_s{j}", align_bytes=64) for j in range(CHUNKS)]
+
+        sig_v = sig_bytes.rearrange("(g m t) k -> g m (t k)", g=GROUPS, t=4)
+        h_v = h.rearrange("(p t) n -> p t n", t=4)
+        b_v = bulk.rearrange("(g p t) n -> g p t n", g=GROUPS, t=4)
+        nc.scalar.dma_start(out=scale[:], in_=sig_scale.rearrange("o (p u e) -> p o u e", u=2, e=2))
+        nc.scalar.dma_start(out=amb[:], in_=ambient.rearrange("(g p t) -> p g t", g=GROUPS, t=4))
+        nc.sync.dma_start(out=codes_in[0][:], in_=sig_v[0])
+        nc.sync.dma_start(out=h_first[:], in_=h_v[:, :, 0:NB])
+        nc.sync.dma_start(out=codes_in[1][:], in_=sig_v[1])
+        nc.sync.dma_start(out=b_first[0][:], in_=b_v[0][:, :, 0:NB])
+        nc.sync.dma_start(out=words[:], in_=norm_words.rearrange("g p n -> p g n"))
+        nc.gpsimd.memset(wsc[:].rearrange("p g n -> p (g n)").bitcast(I32), 0)
+        for q in range(4):
+            nc.sync.dma_start(out=wsc[32 * q : 32 * q + 4, :, :].bitcast(I32),
+                              in_=norm_scales[:, 4 * q : 4 * q + 4, :].rearrange("g q n -> q g n").bitcast(I32))
+        nc.sync.dma_start(out=codes_in[2][:], in_=sig_v[2])
+        nc.sync.dma_start(out=b_first[1][:], in_=b_v[1][:, :, 0:NB])
+        nc.sync.dma_start(out=codes_in[3][:], in_=sig_v[3])
+        nc.sync.dma_start(out=b_first[2][:], in_=b_v[2][:, :, 0:NB])
+        nc.sync.dma_start(out=h_rest[:], in_=h_v[:, :, NB:SAMPLES])
+        nc.sync.dma_start(out=b_first[3][:], in_=b_v[3][:, :, 0:NB])
+        nc.sync.dma_start(out=h_out[:], in_=h.rearrange("(c m) n -> m c n", m=P))
+        for g in range(GROUPS):
+            nc.sync.dma_start(out=b_rest[g][:], in_=b_v[g][:, :, NB:SAMPLES])
+
+        make_identity(nc, ident[:])
+        nc.vector.memset(ones[:], 1.0)
+        nc.scalar.activation(out=junk[:], in_=ones[:], func=ACT.Abs_reciprocal_sqrt)
+
+        wide = {}
+        sg_t = {}
+        xt_t = {}
+
+        def cast(g, half, on_scalar):
+            if half == 0:
+                wide[g] = two.tile([P, 2048], BF16, name="wide", align_bytes=64)
+            cols = slice(1024 * half, 1024 * half + 1024)
+            src = codes_in[g][:, cols].bitcast(F8)
+            if on_scalar:
+                nc.scalar.copy(out=wide[g][:, cols], in_=src)
+            else:
+                nc.vector.tensor_copy(out=wide[g][:, cols], in_=src)
+
+        def turn(g, half):
+            w32 = wide[g][:].bitcast(F32)
+            xt = psum.tile([P, 2, 2, P], F32, name=f"r{half}", tag=f"r{half}")
+            for t2 in range(2):
+                for u in range(2):
+                    base = 256 * (2 * half + t2)
+                    nc.tensor.transpose(xt[:, u, t2, :], w32[:, base + u : base + 256 : 2], ident[:])
+            xt_t[(g, half)] = xt
+
+        def scaled(g, half):
+            if half == 0:
+                sg_t[g] = two.tile([P, 512, 4], BF16, name="sg", align_bytes=64)
+            src = xt_t[(g, half)][:].bitcast(BF16).rearrange("p u t (m e) -> p (t m) u e", e=2)
+            dst = sg_t[g][:, 256 * half : 256 * half + 256, :].rearrange("p r (u e) -> p r u e", u=2)
+            nc.vector.tensor_tensor(out=dst, in0=src, in1=scale[:].to_broadcast([P, 256, 2, 2]), op=MULT)
+
+        def quant_sig(g, half):
+            cols = slice(256 * half, 256 * half + 256)
+            nc.vector.quantize_mx(out=sig_c[g][:, cols].bitcast(E4), scales=sig_s[g][:, cols],
+                                  in_=sg_t[g][:, cols, :].rearrange("p r t -> p (r t)"))
+
+        hi_t = {}
+
+        def h_mix(j, half, on_scalar):
+            if half == 0:
+                hi_t[j] = two.tile([P, NB, 4], BF16, name="hi", align_bytes=64)
+            src = h_first if j == 0 else h_rest
+            n0 = (0 if j == 0 else NB * (j - 1)) + 256 * half
+            i_v = src[:, :, n0 : n0 + 256].rearrange("p t (c i) -> p c t i", i=4)
+            o_v = hi_t[j][:, 256 * half : 256 * half + 256, :].rearrange("p (c i) t -> p c t i", i=4)
+            if on_scalar:
+                nc.scalar.copy(out=o_v, in_=i_v)
+            else:
+                nc.vector.tensor_copy(out=o_v, in_=i_v)
+
+        def h_quant(j):
+            nc.vector.quantize_mx(out=h_c[j][:].bitcast(E4), scales=h_s[j][:], in_=hi_t[j][:].rearrange("p n t -> p (n t)"))
+
+        r_t = {}
+        y_t = {}
+        z_t = {}
+        q_t = {}
+        rc_t = {}
+        rs_t = {}
+        u_t = {}
+
+        def stage1(i):
+            j, g = divmod(i, GROUPS)
+            for t in range(4):
+                r = psum.tile([P, NB], F32, name=f"r{t}", tag=f"r{t}")
+                nc.tensor.matmul_mx(out=r[:], lhsT=sig_c[g][:, P * t : P * t + P].bitcast(E4), lhsT_scale=sig_s[g][:, P * t : P * t + P],
+                                    rhs=h_c[j][:].bitcast(E4), rhs_scale=h_s[j][:], start=True, stop=True)
+                r_t[(i, t)] = r
+
+        def rsqrt(i):
+            g = i % GROUPS
+            y_t[i] = two.tile([P, 4, NB], F32, name="y", align_bytes=64)
+            for t in range(4):
+                nc.scalar.activation(out=y_t[i][:, t, :], in_=r_t[(i, t)][:], func=ACT.Abs_reciprocal_sqrt, bias=amb[:, g, t : t + 1])
+
+        def square(i, half):
+            if half == 0:
+                z_t[i] = three.tile([P, 4, NB], F32, name="z", align_bytes=64)
+            cols = slice(256 * half, 256 * half + 256)
+            if (i, half) in V_SQUARES:
+                return
+            else:
+                nc.scalar.activation(out=z_t[i][:, :, cols], in_=y_t[i][:, :, cols], func=ACT.Square)
+
+        def square_on_vector(i):
+            for half in (0, 1):
+                if (i, half) in V_SQUARES:
+                    cols = slice(256 * half, 256 * half + 256)
+                    nc.vector.tensor_tensor(out=z_t[i][:, :, cols], in0=y_t[i][:, :, cols], in1=y_t[i][:, :, cols], op=MULT)
+
+        def ratio(i, half):
+            j, g = divmod(i, GROUPS)
+            if half == 0:
+                q_t[i] = two.tile([P, NB, 4], BF16, name="q", align_bytes=64)
+            src = b_first[g] if j == 0 else b_rest[g]
+            n0 = (0 if j == 0 else NB * (j - 1)) + 256 * half
+            nc.vector.tensor_tensor(
+                out=q_t[i][:, 256 * half : 256 * half + 256, :].rearrange("p (c i) t -> p c t i", i=4),
+                in0=z_t[i][:, :, 256 * half : 256 * half + 256].rearrange("p t (c i) -> p c t i", i=4),
+                in1=src[:, :, n0 : n0 + 256].rearrange("p t (c i) -> p c t i", i=4), op=MULT)
+
+        def quant_ratio(i, half):
+            if half == 0:
+                rc_t[i] = two.tile([P, NB], U32, name="rc", align_bytes=64)
+                rs_t[i] = two.tile([P, NB], U8, name="rs", align_bytes=64)
+            cols = slice(256 * half, 256 * half + 256)
+            nc.vector.quantize_mx(out=rc_t[i][:, cols].bitcast(E4), scales=rs_t[i][:, cols],
+                                  in_=q_t[i][:, cols, :].rearrange("p n t -> p (n t)"))
+
+        def stage2(i):
+            g = i % GROUPS
+            for c in range(4):
+                if g == 0:
+                    u_t[c] = psum.tile([P, NB], F32, name=f"u{c}", tag=f"u{c}")
+                nc.tensor.matmul_mx(out=u_t[c][:], lhsT=words[:, g, 256 * c : 256 * c + 256].bitcast(E2), lhsT_scale=wsc[:, g, P * c : P * c + P],
+                                    rhs=rc_t[i][:].bitcast(E4), rhs_scale=rs_t[i][:], start=(g == 0), stop=(g == GROUPS - 1))
+
+        out_v = out.rearrange("(c m) n -> m c n", m=P)
+
+        def finish(j, cs):
+            for c in cs:
+                o = three.tile([P, NB], F32, name="o", align_bytes=64)
+                cols = slice(NB * j, NB * j + NB)
+                nc.vector.tensor_tensor(out=o[:], in0=u_t[c][:], in1=h_out[:, c, cols], op=MULT)
+                nc.sync.dma_start(out=out_v[:, c, cols], in_=o[:])
+
+        cast(0, 0, False)
+        cast(0, 1, True)
+        h_mix(0, 0, True)
+        turn(0, 0)
+        turn(0, 1)
+        h_mix(0, 1, False)
+        scaled(0, 0)
+        quant_sig(0, 0)
+        h_quant(0)
+        scaled(0, 1)
+        quant_sig(0, 1)
+        cast(1, 0, False)
+        cast(1, 1, True)
+        stage1(0)
+
+        for i in range(UNITS + 1):
+            j, g = divmod(i, GROUPS)
+            if i < UNITS:
+                rsqrt(i)
+                square(i, 0)
+                square(i, 1)
+            if i + 2 < GROUPS:
+                cast(i + 2, 0, False)
+                cast(i + 2, 1, True)
+            if i in (1, 2):
+                h_mix(1, i - 1, True)
+            if i + 1 < GROUPS:
+                turn(i + 1, 0)
+                turn(i + 1, 1)
+            if i >= GROUPS and i + 1 < UNITS:
+                stage1(i + 1)
+            if i > 0:
+                ratio(i - 1, 0)
+                ratio(i - 1, 1)
+                if i > GROUPS and g == 1:
+                    finish(j - 1, (0, 1))
+                quant_ratio(i - 1, 0)
+                quant_ratio(i - 1, 1)
+                if i > GROUPS and g == 1:
+                    finish(j - 1, (2, 3))
+                stage2(i - 1)
+            if i + 1 < GROUPS:
+                scaled(i + 1, 0)
+                scaled(i + 1, 1)
+                quant_sig(i + 1, 0)
+                quant_sig(i + 1, 1)
+            if i == 3:
+                h_quant(1)
+            if i < GROUPS:
+                stage1(i + 1)
+            if GROUPS <= i < UNITS - GROUPS:
+                if g == 1:
+                    h_mix(j + 1, 0, False)
+                    h_mix(j + 1, 1, False)
+                if g == 2:
+                    h_quant(j + 1)
+            square_on_vector(i)
+        finish(CHUNKS - 1, (0, 1, 2, 3))

@@ -22,7 +22,9 @@ NB = 512
 GROUPS = GENES // 512
 CHUNKS = SAMPLES // NB
 UNITS = GROUPS * CHUNKS
-V_SQUARES = {(5, 1), (9, 1), (13, 1)}
+V_SQUARES = {3: 256, 4: 256, 7: 128, 8: 128, 11: 256, 14: 128}
+V_LEAVES = set()
+LAST_PIECES = [(0, 256), (256, 512)]
 
 
 def tile_deconvolution_multiplicative_update_s13_kernel(tc, sig_bytes, sig_scale, h, ambient, bulk, norm_words, norm_scales, out):
@@ -31,6 +33,7 @@ def tile_deconvolution_multiplicative_update_s13_kernel(tc, sig_bytes, sig_scale
         keep = ctx.enter_context(tc.tile_pool(name="keep", bufs=1))
         two = ctx.enter_context(tc.tile_pool(name="two", bufs=2))
         three = ctx.enter_context(tc.tile_pool(name="three", bufs=3))
+        five = ctx.enter_context(tc.tile_pool(name="five", bufs=5))
         psum = ctx.enter_context(tc.psum_pool(name="psum", bufs=1))
         ctx.enter_context(tc.manual_schedule())
 
@@ -38,6 +41,7 @@ def tile_deconvolution_multiplicative_update_s13_kernel(tc, sig_bytes, sig_scale
         ones = keep.tile([P, 1], F32, name="ones")
         junk = keep.tile([P, 1], F32, name="junk")
         scale = keep.tile([P, 1, 2, 2], F32, name="scale")
+        bscale = keep.tile([P, TYPES], F32, name="bscale")
         amb = keep.tile([P, GROUPS, 4], BF16, name="amb")
         words = keep.tile([P, GROUPS, 1024], U8, name="words", align_bytes=64)
         wsc = keep.tile([P, GROUPS, TYPES], U8, name="wsc", align_bytes=64)
@@ -57,9 +61,11 @@ def tile_deconvolution_multiplicative_update_s13_kernel(tc, sig_bytes, sig_scale
         b_v = bulk.rearrange("(g p t) n -> g p t n", g=GROUPS, t=4)
         nc.scalar.dma_start(out=scale[:], in_=sig_scale.rearrange("o (p u e) -> p o u e", u=2, e=2))
         nc.scalar.dma_start(out=amb[:], in_=ambient.rearrange("(g p t) -> p g t", g=GROUPS, t=4))
-        nc.sync.dma_start(out=codes_in[0][:], in_=sig_v[0])
+        nc.sync.dma_start(out=codes_in[0][:, 0:1024], in_=sig_v[0][:, 0:1024])
         nc.sync.dma_start(out=h_first[:], in_=h_v[:, :, 0:NB])
+        nc.sync.dma_start(out=codes_in[0][:, 1024:2048], in_=sig_v[0][:, 1024:2048])
         nc.sync.dma_start(out=codes_in[1][:], in_=sig_v[1])
+        nc.sync.dma_start(out=bscale[:], in_=sig_scale.rearrange("o k -> (o k)").partition_broadcast(P))
         nc.sync.dma_start(out=b_first[0][:], in_=b_v[0][:, :, 0:NB])
         nc.sync.dma_start(out=words[:], in_=norm_words.rearrange("g p n -> p g n"))
         nc.gpsimd.memset(wsc[:].rearrange("p g n -> p (g n)").bitcast(I32), 0)
@@ -94,6 +100,18 @@ def tile_deconvolution_multiplicative_update_s13_kernel(tc, sig_bytes, sig_scale
             else:
                 nc.vector.tensor_copy(out=wide[g][:, cols], in_=src)
 
+        def product(g):
+            wide[g] = two.tile([P, 2048], BF16, name="wide", align_bytes=64)
+            for t in range(4):
+                row = slice(TYPES * t, TYPES * t + TYPES)
+                nc.vector.tensor_tensor(out=wide[g][:, row], in0=codes_in[g][:, row].bitcast(F8), in1=bscale[:], op=MULT)
+
+        def leave(g, half):
+            if half == 0:
+                sg_t[g] = two.tile([P, 512, 4], BF16, name="sg", align_bytes=64)
+            copy = nc.vector.tensor_copy if (g, half) in V_LEAVES else nc.scalar.copy
+            copy(out=sg_t[g][:, 256 * half : 256 * half + 256, :].bitcast(F32), in_=xt_t[(g, half)][:].rearrange("p u t m -> p (t m) u"))
+
         def turn(g, half):
             w32 = wide[g][:].bitcast(F32)
             xt = psum.tile([P, 2, 2, P], F32, name=f"r{half}", tag=f"r{half}")
@@ -110,22 +128,24 @@ def tile_deconvolution_multiplicative_update_s13_kernel(tc, sig_bytes, sig_scale
             dst = sg_t[g][:, 256 * half : 256 * half + 256, :].rearrange("p r (u e) -> p r u e", u=2)
             nc.vector.tensor_tensor(out=dst, in0=src, in1=scale[:].to_broadcast([P, 256, 2, 2]), op=MULT)
 
-        def quant_sig(g, half):
-            cols = slice(256 * half, 256 * half + 256)
+        def quant_sig(g, half=None):
+            cols = slice(0, 512) if half is None else slice(256 * half, 256 * half + 256)
             nc.vector.quantize_mx(out=sig_c[g][:, cols].bitcast(E4), scales=sig_s[g][:, cols],
                                   in_=sg_t[g][:, cols, :].rearrange("p r t -> p (r t)"))
 
         hi_t = {}
 
-        def h_mix(j, half, on_scalar):
+        def h_mix(j, half, engine):
             if half == 0:
                 hi_t[j] = two.tile([P, NB, 4], BF16, name="hi", align_bytes=64)
             src = h_first if j == 0 else h_rest
             n0 = (0 if j == 0 else NB * (j - 1)) + 256 * half
             i_v = src[:, :, n0 : n0 + 256].rearrange("p t (c i) -> p c t i", i=4)
             o_v = hi_t[j][:, 256 * half : 256 * half + 256, :].rearrange("p (c i) t -> p c t i", i=4)
-            if on_scalar:
+            if engine == "s":
                 nc.scalar.copy(out=o_v, in_=i_v)
+            elif engine == "g":
+                nc.gpsimd.tensor_scalar(out=o_v, in0=i_v, scalar1=1.0, scalar2=0.0, op0=MULT, op1=mybir.AluOpType.add)
             else:
                 nc.vector.tensor_copy(out=o_v, in_=i_v)
 
@@ -154,39 +174,35 @@ def tile_deconvolution_multiplicative_update_s13_kernel(tc, sig_bytes, sig_scale
             for t in range(4):
                 nc.scalar.activation(out=y_t[i][:, t, :], in_=r_t[(i, t)][:], func=ACT.Abs_reciprocal_sqrt, bias=amb[:, g, t : t + 1])
 
-        def square(i, half):
-            if half == 0:
-                z_t[i] = three.tile([P, 4, NB], F32, name="z", align_bytes=64)
-            cols = slice(256 * half, 256 * half + 256)
-            if (i, half) in V_SQUARES:
-                return
-            else:
-                nc.scalar.activation(out=z_t[i][:, :, cols], in_=y_t[i][:, :, cols], func=ACT.Square)
+        def halves(i):
+            return LAST_PIECES if i == UNITS - 1 else [(0, 512)]
+
+        def square(i):
+            z_t[i] = three.tile([P, 4, NB], F32, name="z", align_bytes=64)
+            for a, b in [(0, 512 - V_SQUARES[i])] if i in V_SQUARES else halves(i):
+                nc.scalar.activation(out=z_t[i][:, :, a:b], in_=y_t[i][:, :, a:b], func=ACT.Square)
 
         def square_on_vector(i):
-            for half in (0, 1):
-                if (i, half) in V_SQUARES:
-                    cols = slice(256 * half, 256 * half + 256)
-                    nc.vector.tensor_tensor(out=z_t[i][:, :, cols], in0=y_t[i][:, :, cols], in1=y_t[i][:, :, cols], op=MULT)
+            a = 512 - V_SQUARES[i]
+            nc.vector.tensor_tensor(out=z_t[i][:, :, a:512], in0=y_t[i][:, :, a:512], in1=y_t[i][:, :, a:512], op=MULT)
 
-        def ratio(i, half):
+        def ratio(i):
             j, g = divmod(i, GROUPS)
-            if half == 0:
-                q_t[i] = two.tile([P, NB, 4], BF16, name="q", align_bytes=64)
+            q_t[i] = two.tile([P, NB, 4], BF16, name="q", align_bytes=64)
             src = b_first[g] if j == 0 else b_rest[g]
-            n0 = (0 if j == 0 else NB * (j - 1)) + 256 * half
-            nc.vector.tensor_tensor(
-                out=q_t[i][:, 256 * half : 256 * half + 256, :].rearrange("p (c i) t -> p c t i", i=4),
-                in0=z_t[i][:, :, 256 * half : 256 * half + 256].rearrange("p t (c i) -> p c t i", i=4),
-                in1=src[:, :, n0 : n0 + 256].rearrange("p t (c i) -> p c t i", i=4), op=MULT)
+            n0 = 0 if j == 0 else NB * (j - 1)
+            for a, b in halves(i):
+                nc.vector.tensor_tensor(
+                    out=q_t[i][:, a:b, :].rearrange("p (c i) t -> p c t i", i=4),
+                    in0=z_t[i][:, :, a:b].rearrange("p t (c i) -> p c t i", i=4),
+                    in1=src[:, :, n0 + a : n0 + b].rearrange("p t (c i) -> p c t i", i=4), op=MULT)
 
-        def quant_ratio(i, half):
-            if half == 0:
-                rc_t[i] = two.tile([P, NB], U32, name="rc", align_bytes=64)
-                rs_t[i] = two.tile([P, NB], U8, name="rs", align_bytes=64)
-            cols = slice(256 * half, 256 * half + 256)
-            nc.vector.quantize_mx(out=rc_t[i][:, cols].bitcast(E4), scales=rs_t[i][:, cols],
-                                  in_=q_t[i][:, cols, :].rearrange("p n t -> p (n t)"))
+        def quant_ratio(i):
+            rc_t[i] = two.tile([P, NB], U32, name="rc", align_bytes=64)
+            rs_t[i] = two.tile([P, NB], U8, name="rs", align_bytes=64)
+            for a, b in halves(i):
+                nc.vector.quantize_mx(out=rc_t[i][:, a:b].bitcast(E4), scales=rs_t[i][:, a:b],
+                                      in_=q_t[i][:, a:b, :].rearrange("p n t -> p (n t)"))
 
         def stage2(i):
             g = i % GROUPS
@@ -200,66 +216,62 @@ def tile_deconvolution_multiplicative_update_s13_kernel(tc, sig_bytes, sig_scale
 
         def finish(j, cs):
             for c in cs:
-                o = three.tile([P, NB], F32, name="o", align_bytes=64)
+                o = five.tile([P, NB], F32, name="o", align_bytes=64)
                 cols = slice(NB * j, NB * j + NB)
                 nc.vector.tensor_tensor(out=o[:], in0=u_t[c][:], in1=h_out[:, c, cols], op=MULT)
                 nc.sync.dma_start(out=out_v[:, c, cols], in_=o[:])
 
         cast(0, 0, False)
+        h_mix(0, 0, "s")
         cast(0, 1, True)
-        h_mix(0, 0, True)
         turn(0, 0)
         turn(0, 1)
-        h_mix(0, 1, False)
+        h_mix(0, 1, "g")
         scaled(0, 0)
         quant_sig(0, 0)
         h_quant(0)
         scaled(0, 1)
         quant_sig(0, 1)
-        cast(1, 0, False)
-        cast(1, 1, True)
+        product(1)
         stage1(0)
 
         for i in range(UNITS + 1):
             j, g = divmod(i, GROUPS)
+            first = i < GROUPS
             if i < UNITS:
                 rsqrt(i)
-                square(i, 0)
-                square(i, 1)
-            if i + 2 < GROUPS:
-                cast(i + 2, 0, False)
-                cast(i + 2, 1, True)
-            if i in (1, 2):
-                h_mix(1, i - 1, True)
             if i + 1 < GROUPS:
                 turn(i + 1, 0)
                 turn(i + 1, 1)
-            if i >= GROUPS and i + 1 < UNITS:
+                leave(i + 1, 0)
+                leave(i + 1, 1)
+            if i < UNITS:
+                square(i)
+            if not first and i + 1 < UNITS:
                 stage1(i + 1)
             if i > 0:
-                ratio(i - 1, 0)
-                ratio(i - 1, 1)
-                if i > GROUPS and g == 1:
-                    finish(j - 1, (0, 1))
-                quant_ratio(i - 1, 0)
-                quant_ratio(i - 1, 1)
-                if i > GROUPS and g == 1:
-                    finish(j - 1, (2, 3))
-                stage2(i - 1)
+                ratio(i - 1)
+            if i + 2 < GROUPS:
+                product(i + 2)
             if i + 1 < GROUPS:
-                scaled(i + 1, 0)
-                scaled(i + 1, 1)
-                quant_sig(i + 1, 0)
-                quant_sig(i + 1, 1)
+                quant_sig(i + 1)
+            if i == 2:
+                h_mix(1, 0, "v")
+                h_mix(1, 1, "v")
             if i == 3:
                 h_quant(1)
-            if i < GROUPS:
+            if first:
                 stage1(i + 1)
-            if GROUPS <= i < UNITS - GROUPS:
-                if g == 1:
-                    h_mix(j + 1, 0, False)
-                    h_mix(j + 1, 1, False)
-                if g == 2:
-                    h_quant(j + 1)
-            square_on_vector(i)
+            if i > GROUPS and g == 1:
+                finish(j - 1, (0, 1, 2, 3))
+            if GROUPS <= i < UNITS - GROUPS and g == 2:
+                h_mix(j + 1, 0, "v")
+                h_mix(j + 1, 1, "v")
+            if i in V_SQUARES:
+                square_on_vector(i)
+            if i > 0:
+                quant_ratio(i - 1)
+                stage2(i - 1)
+            if GROUPS <= i < UNITS - GROUPS and g == 2:
+                h_quant(j + 1)
         finish(CHUNKS - 1, (0, 1, 2, 3))

@@ -16,15 +16,26 @@ E4 = mybir.dt.float8_e4m3fn_x4
 E2 = mybir.dt.float4_e2m1fn_x4
 ACT = mybir.ActivationFunctionType
 MULT = mybir.AluOpType.mult
+ADD = mybir.AluOpType.add
 
 P = 128
 NB = 512
 GROUPS = GENES // 512
-CHUNKS = SAMPLES // NB
-UNITS = GROUPS * CHUNKS
-V_SQUARES = {3: 256, 4: 256, 7: 128, 8: 128, 11: 256, 14: 128}
-V_LEAVES = set()
-LAST_PIECES = [(0, 256), (256, 512)]
+CHUNKS = [(0, 512), (512, 512), (1024, 512), (1536, 512)]
+UNITS = GROUPS * len(CHUNKS)
+LAST = 9
+V_SQUARES = {3: 256, 4: 256, 8: 256, 12: 256}
+RUN = 4
+HM = 2
+
+
+def pieces(width):
+    cuts, at = [], 0
+    while at < width:
+        w = max(v for v in (128, 256, 512) if v <= width - at)
+        cuts.append((at, at + w))
+        at += w
+    return cuts
 
 
 def tile_deconvolution_multiplicative_update_s13_kernel(tc, sig_bytes, sig_scale, h, ambient, bulk, norm_words, norm_scales, out):
@@ -33,7 +44,7 @@ def tile_deconvolution_multiplicative_update_s13_kernel(tc, sig_bytes, sig_scale
         keep = ctx.enter_context(tc.tile_pool(name="keep", bufs=1))
         two = ctx.enter_context(tc.tile_pool(name="two", bufs=2))
         three = ctx.enter_context(tc.tile_pool(name="three", bufs=3))
-        five = ctx.enter_context(tc.tile_pool(name="five", bufs=5))
+        four = ctx.enter_context(tc.tile_pool(name="four", bufs=4))
         psum = ctx.enter_context(tc.psum_pool(name="psum", bufs=1))
         ctx.enter_context(tc.manual_schedule())
 
@@ -53,26 +64,24 @@ def tile_deconvolution_multiplicative_update_s13_kernel(tc, sig_bytes, sig_scale
         b_rest = [keep.tile([P, 4, SAMPLES - NB], BF16, name=f"b_rest{g}", align_bytes=64) for g in range(GROUPS)]
         sig_c = [keep.tile([P, 512], U32, name=f"sig_c{g}", align_bytes=64) for g in range(GROUPS)]
         sig_s = [keep.tile([P, 512], U8, name=f"sig_s{g}", align_bytes=64) for g in range(GROUPS)]
-        h_c = [keep.tile([P, NB], U32, name=f"h_c{j}", align_bytes=64) for j in range(CHUNKS)]
-        h_s = [keep.tile([P, NB], U8, name=f"h_s{j}", align_bytes=64) for j in range(CHUNKS)]
+        h_c = [keep.tile([P, NB], U32, name=f"h_c{j}", align_bytes=64) for j in range(4)]
+        h_s = [keep.tile([P, NB], U8, name=f"h_s{j}", align_bytes=64) for j in range(4)]
 
         sig_v = sig_bytes.rearrange("(g m t) k -> g m (t k)", g=GROUPS, t=4)
         h_v = h.rearrange("(p t) n -> p t n", t=4)
         b_v = bulk.rearrange("(g p t) n -> g p t n", g=GROUPS, t=4)
         nc.scalar.dma_start(out=scale[:], in_=sig_scale.rearrange("o (p u e) -> p o u e", u=2, e=2))
         nc.scalar.dma_start(out=amb[:], in_=ambient.rearrange("(g p t) -> p g t", g=GROUPS, t=4))
-        nc.sync.dma_start(out=codes_in[0][:, 0:1024], in_=sig_v[0][:, 0:1024])
+        nc.sync.dma_start(out=codes_in[0][:], in_=sig_v[0])
         nc.sync.dma_start(out=h_first[:], in_=h_v[:, :, 0:NB])
-        nc.sync.dma_start(out=codes_in[0][:, 1024:2048], in_=sig_v[0][:, 1024:2048])
         nc.sync.dma_start(out=codes_in[1][:], in_=sig_v[1])
-        nc.sync.dma_start(out=bscale[:], in_=sig_scale.rearrange("o k -> (o k)").partition_broadcast(P))
+        nc.sync.dma_start(out=codes_in[2][:], in_=sig_v[2])
         nc.sync.dma_start(out=b_first[0][:], in_=b_v[0][:, :, 0:NB])
         nc.sync.dma_start(out=words[:], in_=norm_words.rearrange("g p n -> p g n"))
         nc.gpsimd.memset(wsc[:].rearrange("p g n -> p (g n)").bitcast(I32), 0)
         for q in range(4):
             nc.sync.dma_start(out=wsc[32 * q : 32 * q + 4, :, :].bitcast(I32),
                               in_=norm_scales[:, 4 * q : 4 * q + 4, :].rearrange("g q n -> q g n").bitcast(I32))
-        nc.sync.dma_start(out=codes_in[2][:], in_=sig_v[2])
         nc.sync.dma_start(out=b_first[1][:], in_=b_v[1][:, :, 0:NB])
         nc.sync.dma_start(out=codes_in[3][:], in_=sig_v[3])
         nc.sync.dma_start(out=b_first[2][:], in_=b_v[2][:, :, 0:NB])
@@ -90,27 +99,24 @@ def tile_deconvolution_multiplicative_update_s13_kernel(tc, sig_bytes, sig_scale
         sg_t = {}
         xt_t = {}
 
-        def cast(g, half, on_scalar):
+        def cast(half, engine):
             if half == 0:
-                wide[g] = two.tile([P, 2048], BF16, name="wide", align_bytes=64)
+                wide[0] = two.tile([P, 2048], BF16, name="wide", align_bytes=64)
             cols = slice(1024 * half, 1024 * half + 1024)
-            src = codes_in[g][:, cols].bitcast(F8)
-            if on_scalar:
-                nc.scalar.copy(out=wide[g][:, cols], in_=src)
-            else:
-                nc.vector.tensor_copy(out=wide[g][:, cols], in_=src)
+            copy = nc.scalar.copy if engine == "s" else nc.vector.tensor_copy
+            copy(out=wide[0][:, cols], in_=codes_in[0][:, cols].bitcast(F8))
+
+        def spread_scale():
+            rows = psum.tile([P, 4, P], F32, name="u0", tag="u0")
+            for t in range(4):
+                nc.tensor.matmul(rows[:, t, :], lhsT=scale[:, 0, t // 2, t % 2 : t % 2 + 1].to_broadcast([P, P]), rhs=ident[:], start=True, stop=True)
+            nc.scalar.copy(out=bscale[:].rearrange("p (n t) -> p n t", t=4), in_=rows[:].rearrange("p t n -> p n t"))
 
         def product(g):
             wide[g] = two.tile([P, 2048], BF16, name="wide", align_bytes=64)
             for t in range(4):
                 row = slice(TYPES * t, TYPES * t + TYPES)
                 nc.vector.tensor_tensor(out=wide[g][:, row], in0=codes_in[g][:, row].bitcast(F8), in1=bscale[:], op=MULT)
-
-        def leave(g, half):
-            if half == 0:
-                sg_t[g] = two.tile([P, 512, 4], BF16, name="sg", align_bytes=64)
-            copy = nc.vector.tensor_copy if (g, half) in V_LEAVES else nc.scalar.copy
-            copy(out=sg_t[g][:, 256 * half : 256 * half + 256, :].bitcast(F32), in_=xt_t[(g, half)][:].rearrange("p u t m -> p (t m) u"))
 
         def turn(g, half):
             w32 = wide[g][:].bitcast(F32)
@@ -121,15 +127,21 @@ def tile_deconvolution_multiplicative_update_s13_kernel(tc, sig_bytes, sig_scale
                     nc.tensor.transpose(xt[:, u, t2, :], w32[:, base + u : base + 256 : 2], ident[:])
             xt_t[(g, half)] = xt
 
-        def scaled(g, half):
+        def leave(g, half):
             if half == 0:
                 sg_t[g] = two.tile([P, 512, 4], BF16, name="sg", align_bytes=64)
-            src = xt_t[(g, half)][:].bitcast(BF16).rearrange("p u t (m e) -> p (t m) u e", e=2)
-            dst = sg_t[g][:, 256 * half : 256 * half + 256, :].rearrange("p r (u e) -> p r u e", u=2)
-            nc.vector.tensor_tensor(out=dst, in0=src, in1=scale[:].to_broadcast([P, 256, 2, 2]), op=MULT)
+            nc.scalar.copy(out=sg_t[g][:, 256 * half : 256 * half + 256, :].bitcast(F32), in_=xt_t[(g, half)][:].rearrange("p u t m -> p (t m) u"))
 
-        def quant_sig(g, half=None):
-            cols = slice(0, 512) if half is None else slice(256 * half, 256 * half + 256)
+        def scaled(t0, t1):
+            if t0 == 0:
+                sg_t[0] = two.tile([P, 512, 4], BF16, name="sg", align_bytes=64)
+            half = t0 // 2
+            src = xt_t[(0, half)][:, :, t0 - 2 * half : t1 - 2 * half, :].bitcast(BF16).rearrange("p u t (m e) -> p (t m) u e", e=2)
+            dst = sg_t[0][:, P * t0 : P * t1, :].rearrange("p r (u e) -> p r u e", u=2)
+            nc.vector.tensor_tensor(out=dst, in0=src, in1=scale[:].to_broadcast([P, P * (t1 - t0), 2, 2]), op=MULT)
+
+        def quant_sig(g, t0, t1):
+            cols = slice(P * t0, P * t1)
             nc.vector.quantize_mx(out=sig_c[g][:, cols].bitcast(E4), scales=sig_s[g][:, cols],
                                   in_=sg_t[g][:, cols, :].rearrange("p r t -> p (r t)"))
 
@@ -140,12 +152,12 @@ def tile_deconvolution_multiplicative_update_s13_kernel(tc, sig_bytes, sig_scale
                 hi_t[j] = two.tile([P, NB, 4], BF16, name="hi", align_bytes=64)
             src = h_first if j == 0 else h_rest
             n0 = (0 if j == 0 else NB * (j - 1)) + 256 * half
-            i_v = src[:, :, n0 : n0 + 256].rearrange("p t (c i) -> p c t i", i=4)
-            o_v = hi_t[j][:, 256 * half : 256 * half + 256, :].rearrange("p (c i) t -> p c t i", i=4)
+            i_v = src[:, :, n0 : n0 + 256].rearrange("p t (c i) -> p c t i", i=RUN)
+            o_v = hi_t[j][:, 256 * half : 256 * half + 256, :].rearrange("p (c i) t -> p c t i", i=RUN)
             if engine == "s":
                 nc.scalar.copy(out=o_v, in_=i_v)
             elif engine == "g":
-                nc.gpsimd.tensor_scalar(out=o_v, in0=i_v, scalar1=1.0, scalar2=0.0, op0=MULT, op1=mybir.AluOpType.add)
+                nc.gpsimd.tensor_scalar(out=o_v, in0=i_v, scalar1=1.0, scalar2=0.0, op0=MULT, op1=ADD)
             else:
                 nc.vector.tensor_copy(out=o_v, in_=i_v)
 
@@ -160,118 +172,165 @@ def tile_deconvolution_multiplicative_update_s13_kernel(tc, sig_bytes, sig_scale
         rs_t = {}
         u_t = {}
 
-        def stage1(i):
+        def spot(i):
             j, g = divmod(i, GROUPS)
-            for t in range(4):
-                r = psum.tile([P, NB], F32, name=f"r{t}", tag=f"r{t}")
-                nc.tensor.matmul_mx(out=r[:], lhsT=sig_c[g][:, P * t : P * t + P].bitcast(E4), lhsT_scale=sig_s[g][:, P * t : P * t + P],
-                                    rhs=h_c[j][:].bitcast(E4), rhs_scale=h_s[j][:], start=True, stop=True)
-                r_t[(i, t)] = r
+            n0, width = CHUNKS[j]
+            return j, g, n0, width
+
+        def stage1(i, ts=(0, 1, 2, 3)):
+            j, g, n0, width = spot(i)
+            hq, off = n0 // NB, n0 % NB
+            if j == LAST:
+                bank = psum.tile([P, 4, P], F32, name=f"r{g}", tag=f"r{g}")
+            for t in ts:
+                if j == LAST:
+                    r_t[(i, t)] = bank[:, t, :]
+                else:
+                    rt = psum.tile([P, width], F32, name=f"r{t}", tag=f"r{t}")
+                    r_t[(i, t)] = rt[:]
+                for a, b in pieces(width):
+                    nc.tensor.matmul_mx(out=r_t[(i, t)][:, a:b], lhsT=sig_c[g][:, P * t : P * t + P].bitcast(E4), lhsT_scale=sig_s[g][:, P * t : P * t + P],
+                                        rhs=h_c[hq][:, off + a : off + b].bitcast(E4), rhs_scale=h_s[hq][:, off + a : off + b], start=True, stop=True)
 
         def rsqrt(i):
-            g = i % GROUPS
-            y_t[i] = two.tile([P, 4, NB], F32, name="y", align_bytes=64)
+            j, g, n0, width = spot(i)
+            y_t[i] = two.tile([P, 4, width], F32, name="y", align_bytes=64)
             for t in range(4):
-                nc.scalar.activation(out=y_t[i][:, t, :], in_=r_t[(i, t)][:], func=ACT.Abs_reciprocal_sqrt, bias=amb[:, g, t : t + 1])
+                nc.scalar.activation(out=y_t[i][:, t, :], in_=r_t[(i, t)], func=ACT.Abs_reciprocal_sqrt, bias=amb[:, g, t : t + 1])
 
-        def halves(i):
-            return LAST_PIECES if i == UNITS - 1 else [(0, 512)]
+        def parts(i, width):
+            return [(0, 256), (256, 512)] if i == UNITS - 1 else [(0, width)]
 
         def square(i):
-            z_t[i] = three.tile([P, 4, NB], F32, name="z", align_bytes=64)
-            for a, b in [(0, 512 - V_SQUARES[i])] if i in V_SQUARES else halves(i):
-                nc.scalar.activation(out=z_t[i][:, :, a:b], in_=y_t[i][:, :, a:b], func=ACT.Square)
+            width = spot(i)[3]
+            z_t[i] = three.tile([P, 4, width], F32, name="z", align_bytes=64)
+            b = width - V_SQUARES.get(i, 0)
+            for lo, hi in parts(i, b):
+                nc.scalar.activation(out=z_t[i][:, :, lo:hi], in_=y_t[i][:, :, lo:hi], func=ACT.Square)
 
         def square_on_vector(i):
-            a = 512 - V_SQUARES[i]
-            nc.vector.tensor_tensor(out=z_t[i][:, :, a:512], in0=y_t[i][:, :, a:512], in1=y_t[i][:, :, a:512], op=MULT)
+            width = spot(i)[3]
+            a = width - V_SQUARES[i]
+            nc.vector.tensor_tensor(out=z_t[i][:, :, a:width], in0=y_t[i][:, :, a:width], in1=y_t[i][:, :, a:width], op=MULT)
 
         def ratio(i):
-            j, g = divmod(i, GROUPS)
-            q_t[i] = two.tile([P, NB, 4], BF16, name="q", align_bytes=64)
+            j, g, n0, width = spot(i)
+            q_t[i] = three.tile([P, width, 4], BF16, name="q", align_bytes=64)
             src = b_first[g] if j == 0 else b_rest[g]
-            n0 = 0 if j == 0 else NB * (j - 1)
-            for a, b in halves(i):
+            s0 = n0 if j == 0 else n0 - NB
+            for a, b in parts(i, width):
                 nc.vector.tensor_tensor(
-                    out=q_t[i][:, a:b, :].rearrange("p (c i) t -> p c t i", i=4),
-                    in0=z_t[i][:, :, a:b].rearrange("p t (c i) -> p c t i", i=4),
-                    in1=src[:, :, n0 + a : n0 + b].rearrange("p t (c i) -> p c t i", i=4), op=MULT)
+                    out=q_t[i][:, a:b, :].rearrange("p (c i) t -> p c t i", i=RUN),
+                    in0=z_t[i][:, :, a:b].rearrange("p t (c i) -> p c t i", i=RUN),
+                    in1=src[:, :, s0 + a : s0 + b].rearrange("p t (c i) -> p c t i", i=RUN), op=MULT)
 
         def quant_ratio(i):
-            rc_t[i] = two.tile([P, NB], U32, name="rc", align_bytes=64)
-            rs_t[i] = two.tile([P, NB], U8, name="rs", align_bytes=64)
-            for a, b in halves(i):
+            width = spot(i)[3]
+            rc_t[i] = four.tile([P, width], U32, name="rc", align_bytes=64)
+            rs_t[i] = four.tile([P, width], U8, name="rs", align_bytes=64)
+            for a, b in parts(i, width):
                 nc.vector.quantize_mx(out=rc_t[i][:, a:b].bitcast(E4), scales=rs_t[i][:, a:b],
                                       in_=q_t[i][:, a:b, :].rearrange("p n t -> p (n t)"))
 
-        def stage2(i):
+        def pass2(i, c, acc, a, b):
             g = i % GROUPS
-            for c in range(4):
-                if g == 0:
-                    u_t[c] = psum.tile([P, NB], F32, name=f"u{c}", tag=f"u{c}")
-                nc.tensor.matmul_mx(out=u_t[c][:], lhsT=words[:, g, 256 * c : 256 * c + 256].bitcast(E2), lhsT_scale=wsc[:, g, P * c : P * c + P],
-                                    rhs=rc_t[i][:].bitcast(E4), rhs_scale=rs_t[i][:], start=(g == 0), stop=(g == GROUPS - 1))
+            nc.tensor.matmul_mx(out=acc[:, a:b], lhsT=words[:, g, 256 * c : 256 * c + 256].bitcast(E2), lhsT_scale=wsc[:, g, P * c : P * c + P],
+                                rhs=rc_t[i][:, a:b].bitcast(E4), rhs_scale=rs_t[i][:, a:b], start=(g == 0), stop=(g == GROUPS - 1))
+
+        def stage2(i):
+            j, g, n0, width = spot(i)
+            if width in (P, NB):
+                for c in range(4):
+                    if g == 0:
+                        bank = f"r{c}" if j == LAST else f"u{c}"
+                        acc = psum.tile([P, width], F32, name=bank, tag=bank)
+                        u_t[c] = acc
+                    pass2(i, c, u_t[c], 0, width)
+            elif g == GROUPS - 1:
+                for c in range(4):
+                    acc = psum.tile([P, width], F32, name=f"u{c}", tag=f"u{c}")
+                    for a in range(0, width, P):
+                        for k in range(GROUPS):
+                            pass2(i - GROUPS + 1 + k, c, acc, a, a + P)
+                    u_t[c] = acc
 
         out_v = out.rearrange("(c m) n -> m c n", m=P)
+        o_t = {}
 
-        def finish(j, cs):
-            for c in cs:
-                o = five.tile([P, NB], F32, name="o", align_bytes=64)
-                cols = slice(NB * j, NB * j + NB)
+        def finish(j, c):
+            n0, width = CHUNKS[j]
+            cols = slice(n0, n0 + width)
+            if j == LAST:
+                if c == 0:
+                    o_t[0] = keep.tile([P, 4, width], F32, name="o_last")
+                nc.vector.tensor_tensor(out=o_t[0][:, c, :], in0=u_t[c][:], in1=h_out[:, c, cols], op=MULT)
+                if c % 2:
+                    nc.sync.dma_start(out=out_v[:, c - 1 : c + 1, cols], in_=o_t[0][:, c - 1 : c + 1, :])
+            else:
+                o = four.tile([P, width], F32, name="o", align_bytes=64)
                 nc.vector.tensor_tensor(out=o[:], in0=u_t[c][:], in1=h_out[:, c, cols], op=MULT)
                 nc.sync.dma_start(out=out_v[:, c, cols], in_=o[:])
 
-        cast(0, 0, False)
-        h_mix(0, 0, "s")
-        cast(0, 1, True)
+        cast(0, "v")
         turn(0, 0)
-        turn(0, 1)
+        cast(1, "s")
+        h_mix(0, 0, "s")
         h_mix(0, 1, "g")
-        scaled(0, 0)
-        quant_sig(0, 0)
-        h_quant(0)
         scaled(0, 1)
-        quant_sig(0, 1)
+        scaled(1, 2)
+        quant_sig(0, 0, 2)
+        turn(0, 1)
+        spread_scale()
+        h_quant(0)
+        stage1(0, (0, 1))
+        scaled(2, 4)
+        quant_sig(0, 2, 4)
+        stage1(0, (2, 3))
         product(1)
-        stage1(0)
 
-        for i in range(UNITS + 1):
+        for i in range(UNITS):
             j, g = divmod(i, GROUPS)
             first = i < GROUPS
-            if i < UNITS:
-                rsqrt(i)
+            rsqrt(i)
             if i + 1 < GROUPS:
                 turn(i + 1, 0)
                 turn(i + 1, 1)
                 leave(i + 1, 0)
                 leave(i + 1, 1)
-            if i < UNITS:
-                square(i)
+            square(i)
             if not first and i + 1 < UNITS:
                 stage1(i + 1)
-            if i > 0:
-                ratio(i - 1)
-            if i + 2 < GROUPS:
-                product(i + 2)
-            if i + 1 < GROUPS:
-                quant_sig(i + 1)
-            if i == 2:
-                h_mix(1, 0, "v")
-                h_mix(1, 1, "v")
-            if i == 3:
-                h_quant(1)
-            if first:
-                stage1(i + 1)
-            if i > GROUPS and g == 1:
-                finish(j - 1, (0, 1, 2, 3))
-            if GROUPS <= i < UNITS - GROUPS and g == 2:
+            for step in ("DQPHEV" if first else "DFVE"):
+                if step == "D" and i > 0:
+                    ratio(i - 1)
+                if step == "P" and i + 2 < GROUPS:
+                    product(i + 2)
+                if step == "H" and i == HM:
+                    h_mix(1, 0, "v")
+                    h_mix(1, 1, "v")
+                if step == "Q":
+                    if i == 3:
+                        h_quant(1)
+                    else:
+                        quant_sig(i + 1, 0, 4)
+                    stage1(i + 1)
+                if step == "F" and i > GROUPS and g == 2:
+                    for c in range(4):
+                        finish(j - 1, c)
+                if step == "V" and i in V_SQUARES:
+                    square_on_vector(i)
+                if step == "E" and i > 1:
+                    quant_ratio(i - 2)
+                    stage2(i - 2)
+            if j in (1, 2) and g == 1:
                 h_mix(j + 1, 0, "v")
                 h_mix(j + 1, 1, "v")
-            if i in V_SQUARES:
-                square_on_vector(i)
-            if i > 0:
-                quant_ratio(i - 1)
-                stage2(i - 1)
-            if GROUPS <= i < UNITS - GROUPS and g == 2:
+            if j in (1, 2) and g == 2:
                 h_quant(j + 1)
-        finish(CHUNKS - 1, (0, 1, 2, 3))
+        quant_ratio(UNITS - 2)
+        stage2(UNITS - 2)
+        ratio(UNITS - 1)
+        quant_ratio(UNITS - 1)
+        stage2(UNITS - 1)
+        for c in range(4):
+            finish(3, c)

@@ -220,9 +220,9 @@ def tile_deconvolution_multiplicative_update_s13_kernel(tc, sig_bytes, sig_scale
             s0 = n0 if j == 0 else n0 - NB
             for a, b in parts(i, width):
                 nc.vector.tensor_tensor(
-                    out=q_t[i][:, a:b, :].rearrange("p (c i) t -> p c t i", i=RUN),
-                    in0=z_t[i][:, :, a:b].rearrange("p t (c i) -> p c t i", i=RUN),
-                    in1=src[:, :, s0 + a : s0 + b].rearrange("p t (c i) -> p c t i", i=RUN), op=MULT)
+                    out=q_t[i][:, a:b, :].rearrange("p (c i) t -> p c t i", i=8),
+                    in0=z_t[i][:, :, a:b].rearrange("p t (c i) -> p c t i", i=8),
+                    in1=src[:, :, s0 + a : s0 + b].rearrange("p t (c i) -> p c t i", i=8), op=MULT)
 
         def quant_ratio(i):
             width = spot(i)[3]

from contextlib import ExitStack

import concourse.mybir as mybir
from concourse.masks import make_identity

GENES, TYPES, SAMPLES = 2048, 512, 2048
FLOPS = 2 * 2 * GENES * TYPES * SAMPLES

F32 = mybir.dt.float32
BF16 = mybir.dt.bfloat16
U32 = mybir.dt.uint32
I32 = mybir.dt.int32
U8 = mybir.dt.uint8
F8 = mybir.dt.float8_e4m3fn
E4 = mybir.dt.float8_e4m3fn_x4
E2 = mybir.dt.float4_e2m1fn_x4
ACT = mybir.ActivationFunctionType
MULT = mybir.AluOpType.mult
ADD = mybir.AluOpType.add

P = 128
NB = 512
GROUPS = GENES // 512
CHUNKS = [(0, 512), (512, 512), (1024, 512), (1536, 512)]
UNITS = GROUPS * len(CHUNKS)
LAST = 9
V_SQUARES = {3: 256, 4: 256, 8: 256, 12: 256}
RUN = 4
HM = 2


def pieces(width):
    cuts, at = [], 0
    while at < width:
        w = max(v for v in (128, 256, 512) if v <= width - at)
        cuts.append((at, at + w))
        at += w
    return cuts


def tile_deconvolution_multiplicative_update_s13_kernel(tc, sig_bytes, sig_scale, h, ambient, bulk, norm_words, norm_scales, out):
    nc = tc.nc
    with ExitStack() as ctx:
        keep = ctx.enter_context(tc.tile_pool(name="keep", bufs=1))
        two = ctx.enter_context(tc.tile_pool(name="two", bufs=2))
        three = ctx.enter_context(tc.tile_pool(name="three", bufs=3))
        four = ctx.enter_context(tc.tile_pool(name="four", bufs=4))
        psum = ctx.enter_context(tc.psum_pool(name="psum", bufs=1))
        ctx.enter_context(tc.manual_schedule())

        ident = keep.tile([P, P], F32, name="ident")
        ones = keep.tile([P, 1], F32, name="ones")
        junk = keep.tile([P, 1], F32, name="junk")
        scale = keep.tile([P, 1, 2, 2], F32, name="scale")
        bscale = keep.tile([P, TYPES], F32, name="bscale")
        amb = keep.tile([P, GROUPS, 4], BF16, name="amb")
        words = keep.tile([P, GROUPS, 1024], U8, name="words", align_bytes=64)
        wsc = keep.tile([P, GROUPS, TYPES], U8, name="wsc", align_bytes=64)
        codes_in = [keep.tile([P, 2048], U8, name=f"sigraw{g}", align_bytes=64) for g in range(GROUPS)]
        h_first = keep.tile([P, 4, NB], BF16, name="h_first", align_bytes=64)
        h_rest = keep.tile([P, 4, SAMPLES - NB], BF16, name="h_rest", align_bytes=64)
        h_out = keep.tile([P, 4, SAMPLES], BF16, name="h_out", align_bytes=64)
        b_first = [keep.tile([P, 4, NB], BF16, name=f"b_first{g}", align_bytes=64) for g in range(GROUPS)]
        b_rest = [keep.tile([P, 4, SAMPLES - NB], BF16, name=f"b_rest{g}", align_bytes=64) for g in range(GROUPS)]
        sig_c = [keep.tile([P, 512], U32, name=f"sig_c{g}", align_bytes=64) for g in range(GROUPS)]
        sig_s = [keep.tile([P, 512], U8, name=f"sig_s{g}", align_bytes=64) for g in range(GROUPS)]
        h_c = [keep.tile([P, NB], U32, name=f"h_c{j}", align_bytes=64) for j in range(4)]
        h_s = [keep.tile([P, NB], U8, name=f"h_s{j}", align_bytes=64) for j in range(4)]

        sig_v = sig_bytes.rearrange("(g m t) k -> g m (t k)", g=GROUPS, t=4)
        h_v = h.rearrange("(p t) n -> p t n", t=4)
        b_v = bulk.rearrange("(g p t) n -> g p t n", g=GROUPS, t=4)
        nc.scalar.dma_start(out=scale[:], in_=sig_scale.rearrange("o (p u e) -> p o u e", u=2, e=2))
        nc.scalar.dma_start(out=amb[:], in_=ambient.rearrange("(g p t) -> p g t", g=GROUPS, t=4))
        nc.sync.dma_start(out=codes_in[0][:], in_=sig_v[0])
        nc.sync.dma_start(out=h_first[:], in_=h_v[:, :, 0:NB])
        nc.sync.dma_start(out=codes_in[1][:], in_=sig_v[1])
        nc.sync.dma_start(out=codes_in[2][:], in_=sig_v[2])
        nc.sync.dma_start(out=b_first[0][:], in_=b_v[0][:, :, 0:NB])
        nc.sync.dma_start(out=words[:], in_=norm_words.rearrange("g p n -> p g n"))
        nc.gpsimd.memset(wsc[:].rearrange("p g n -> p (g n)").bitcast(I32), 0)
        for q in range(4):
            nc.sync.dma_start(out=wsc[32 * q : 32 * q + 4, :, :].bitcast(I32),
                              in_=norm_scales[:, 4 * q : 4 * q + 4, :].rearrange("g q n -> q g n").bitcast(I32))
        nc.sync.dma_start(out=b_first[1][:], in_=b_v[1][:, :, 0:NB])
        nc.sync.dma_start(out=codes_in[3][:], in_=sig_v[3])
        nc.sync.dma_start(out=b_first[2][:], in_=b_v[2][:, :, 0:NB])
        nc.sync.dma_start(out=h_rest[:], in_=h_v[:, :, NB:SAMPLES])
        nc.sync.dma_start(out=b_first[3][:], in_=b_v[3][:, :, 0:NB])
        nc.sync.dma_start(out=h_out[:], in_=h.rearrange("(c m) n -> m c n", m=P))
        for g in range(GROUPS):
            nc.sync.dma_start(out=b_rest[g][:], in_=b_v[g][:, :, NB:SAMPLES])

        make_identity(nc, ident[:])
        nc.vector.memset(ones[:], 1.0)
        nc.scalar.activation(out=junk[:], in_=ones[:], func=ACT.Abs_reciprocal_sqrt)

        wide = {}
        sg_t = {}
        xt_t = {}

        def cast(half, engine):
            if half == 0:
                wide[0] = two.tile([P, 2048], BF16, name="wide", align_bytes=64)
            cols = slice(1024 * half, 1024 * half + 1024)
            copy = nc.scalar.copy if engine == "s" else nc.vector.tensor_copy
            copy(out=wide[0][:, cols], in_=codes_in[0][:, cols].bitcast(F8))

        def spread_scale():
            rows = psum.tile([P, 4, P], F32, name="u0", tag="u0")
            for t in range(4):
                nc.tensor.matmul(rows[:, t, :], lhsT=scale[:, 0, t // 2, t % 2 : t % 2 + 1].to_broadcast([P, P]), rhs=ident[:], start=True, stop=True)
            nc.scalar.copy(out=bscale[:].rearrange("p (n t) -> p n t", t=4), in_=rows[:].rearrange("p t n -> p n t"))

        def product(g):
            wide[g] = two.tile([P, 2048], BF16, name="wide", align_bytes=64)
            for t in range(4):
                row = slice(TYPES * t, TYPES * t + TYPES)
                nc.vector.tensor_tensor(out=wide[g][:, row], in0=codes_in[g][:, row].bitcast(F8), in1=bscale[:], op=MULT)

        def turn(g, half):
            w32 = wide[g][:].bitcast(F32)
            xt = psum.tile([P, 2, 2, P], F32, name=f"r{half}", tag=f"r{half}")
            for t2 in range(2):
                for u in range(2):
                    base = 256 * (2 * half + t2)
                    nc.tensor.transpose(xt[:, u, t2, :], w32[:, base + u : base + 256 : 2], ident[:])
            xt_t[(g, half)] = xt

        def leave(g, half):
            if half == 0:
                sg_t[g] = two.tile([P, 512, 4], BF16, name="sg", align_bytes=64)
            nc.scalar.copy(out=sg_t[g][:, 256 * half : 256 * half + 256, :].bitcast(F32), in_=xt_t[(g, half)][:].rearrange("p u t m -> p (t m) u"))

        def scaled(t0, t1):
            if t0 == 0:
                sg_t[0] = two.tile([P, 512, 4], BF16, name="sg", align_bytes=64)
            half = t0 // 2
            src = xt_t[(0, half)][:, :, t0 - 2 * half : t1 - 2 * half, :].bitcast(BF16).rearrange("p u t (m e) -> p (t m) u e", e=2)
            dst = sg_t[0][:, P * t0 : P * t1, :].rearrange("p r (u e) -> p r u e", u=2)
            nc.vector.tensor_tensor(out=dst, in0=src, in1=scale[:].to_broadcast([P, P * (t1 - t0), 2, 2]), op=MULT)

        def quant_sig(g, t0, t1):
            cols = slice(P * t0, P * t1)
            nc.vector.quantize_mx(out=sig_c[g][:, cols].bitcast(E4), scales=sig_s[g][:, cols],
                                  in_=sg_t[g][:, cols, :].rearrange("p r t -> p (r t)"))

        hi_t = {}

        def h_mix(j, half, engine):
            if half == 0:
                hi_t[j] = two.tile([P, NB, 4], BF16, name="hi", align_bytes=64)
            src = h_first if j == 0 else h_rest
            n0 = (0 if j == 0 else NB * (j - 1)) + 256 * half
            i_v = src[:, :, n0 : n0 + 256].rearrange("p t (c i) -> p c t i", i=RUN)
            o_v = hi_t[j][:, 256 * half : 256 * half + 256, :].rearrange("p (c i) t -> p c t i", i=RUN)
            if engine == "s":
                nc.scalar.copy(out=o_v, in_=i_v)
            elif engine == "g":
                nc.gpsimd.tensor_scalar(out=o_v, in0=i_v, scalar1=1.0, scalar2=0.0, op0=MULT, op1=ADD)
            else:
                nc.vector.tensor_copy(out=o_v, in_=i_v)

        def h_quant(j):
            nc.vector.quantize_mx(out=h_c[j][:].bitcast(E4), scales=h_s[j][:], in_=hi_t[j][:].rearrange("p n t -> p (n t)"))

        r_t = {}
        y_t = {}
        z_t = {}
        q_t = {}
        rc_t = {}
        rs_t = {}
        u_t = {}

        def spot(i):
            j, g = divmod(i, GROUPS)
            n0, width = CHUNKS[j]
            return j, g, n0, width

        def stage1(i, ts=(0, 1, 2, 3)):
            j, g, n0, width = spot(i)
            hq, off = n0 // NB, n0 % NB
            if j == LAST:
                bank = psum.tile([P, 4, P], F32, name=f"r{g}", tag=f"r{g}")
            for t in ts:
                if j == LAST:
                    r_t[(i, t)] = bank[:, t, :]
                else:
                    rt = psum.tile([P, width], F32, name=f"r{t}", tag=f"r{t}")
                    r_t[(i, t)] = rt[:]
                for a, b in pieces(width):
                    nc.tensor.matmul_mx(out=r_t[(i, t)][:, a:b], lhsT=sig_c[g][:, P * t : P * t + P].bitcast(E4), lhsT_scale=sig_s[g][:, P * t : P * t + P],
                                        rhs=h_c[hq][:, off + a : off + b].bitcast(E4), rhs_scale=h_s[hq][:, off + a : off + b], start=True, stop=True)

        def rsqrt(i):
            j, g, n0, width = spot(i)
            y_t[i] = two.tile([P, 4, width], F32, name="y", align_bytes=64)
            for t in range(4):
                nc.scalar.activation(out=y_t[i][:, t, :], in_=r_t[(i, t)], func=ACT.Abs_reciprocal_sqrt, bias=amb[:, g, t : t + 1])

        def parts(i, width):
            return [(0, 256), (256, 512)] if i == UNITS - 1 else [(0, width)]

        def square(i):
            width = spot(i)[3]
            z_t[i] = three.tile([P, 4, width], F32, name="z", align_bytes=64)
            b = width - V_SQUARES.get(i, 0)
            for lo, hi in parts(i, b):
                nc.scalar.activation(out=z_t[i][:, :, lo:hi], in_=y_t[i][:, :, lo:hi], func=ACT.Square)

        def square_on_vector(i):
            width = spot(i)[3]
            a = width - V_SQUARES[i]
            nc.vector.tensor_tensor(out=z_t[i][:, :, a:width], in0=y_t[i][:, :, a:width], in1=y_t[i][:, :, a:width], op=MULT)

        def ratio(i):
            j, g, n0, width = spot(i)
            q_t[i] = three.tile([P, width, 4], BF16, name="q", align_bytes=64)
            src = b_first[g] if j == 0 else b_rest[g]
            s0 = n0 if j == 0 else n0 - NB
            for a, b in parts(i, width):
                nc.vector.tensor_tensor(
                    out=q_t[i][:, a:b, :].rearrange("p (c i) t -> p c t i", i=8),
                    in0=z_t[i][:, :, a:b].rearrange("p t (c i) -> p c t i", i=8),
                    in1=src[:, :, s0 + a : s0 + b].rearrange("p t (c i) -> p c t i", i=8), op=MULT)

        def quant_ratio(i):
            width = spot(i)[3]
            rc_t[i] = four.tile([P, width], U32, name="rc", align_bytes=64)
            rs_t[i] = four.tile([P, width], U8, name="rs", align_bytes=64)
            for a, b in parts(i, width):
                nc.vector.quantize_mx(out=rc_t[i][:, a:b].bitcast(E4), scales=rs_t[i][:, a:b],
                                      in_=q_t[i][:, a:b, :].rearrange("p n t -> p (n t)"))

        def pass2(i, c, acc, a, b):
            g = i % GROUPS
            nc.tensor.matmul_mx(out=acc[:, a:b], lhsT=words[:, g, 256 * c : 256 * c + 256].bitcast(E2), lhsT_scale=wsc[:, g, P * c : P * c + P],
                                rhs=rc_t[i][:, a:b].bitcast(E4), rhs_scale=rs_t[i][:, a:b], start=(g == 0), stop=(g == GROUPS - 1))

        def stage2(i):
            j, g, n0, width = spot(i)
            if width in (P, NB):
                for c in range(4):
                    if g == 0:
                        bank = f"r{c}" if j == LAST else f"u{c}"
                        acc = psum.tile([P, width], F32, name=bank, tag=bank)
                        u_t[c] = acc
                    pass2(i, c, u_t[c], 0, width)
            elif g == GROUPS - 1:
                for c in range(4):
                    acc = psum.tile([P, width], F32, name=f"u{c}", tag=f"u{c}")
                    for a in range(0, width, P):
                        for k in range(GROUPS):
                            pass2(i - GROUPS + 1 + k, c, acc, a, a + P)
                    u_t[c] = acc

        out_v = out.rearrange("(c m) n -> m c n", m=P)
        o_t = {}

        def finish(j, c):
            n0, width = CHUNKS[j]
            cols = slice(n0, n0 + width)
            if j == LAST:
                if c == 0:
                    o_t[0] = keep.tile([P, 4, width], F32, name="o_last")
                nc.vector.tensor_tensor(out=o_t[0][:, c, :], in0=u_t[c][:], in1=h_out[:, c, cols], op=MULT)
                if c % 2:
                    nc.sync.dma_start(out=out_v[:, c - 1 : c + 1, cols], in_=o_t[0][:, c - 1 : c + 1, :])
            else:
                o = four.tile([P, width], F32, name="o", align_bytes=64)
                nc.vector.tensor_tensor(out=o[:], in0=u_t[c][:], in1=h_out[:, c, cols], op=MULT)
                nc.sync.dma_start(out=out_v[:, c, cols], in_=o[:])

        cast(0, "v")
        turn(0, 0)
        cast(1, "s")
        h_mix(0, 0, "s")
        h_mix(0, 1, "g")
        scaled(0, 1)
        scaled(1, 2)
        quant_sig(0, 0, 2)
        turn(0, 1)
        spread_scale()
        h_quant(0)
        stage1(0, (0, 1))
        scaled(2, 4)
        quant_sig(0, 2, 4)
        stage1(0, (2, 3))
        product(1)

        for i in range(UNITS):
            j, g = divmod(i, GROUPS)
            first = i < GROUPS
            rsqrt(i)
            if i + 1 < GROUPS:
                turn(i + 1, 0)
                turn(i + 1, 1)
                leave(i + 1, 0)
                leave(i + 1, 1)
            square(i)
            if not first and i + 1 < UNITS:
                stage1(i + 1)
            for step in ("DQPHEV" if first else "DFVE"):
                if step == "D" and i > 0:
                    ratio(i - 1)
                if step == "P" and i + 2 < GROUPS:
                    product(i + 2)
                if step == "H" and i == HM:
                    h_mix(1, 0, "v")
                    h_mix(1, 1, "v")
                if step == "Q":
                    if i == 3:
                        h_quant(1)
                    else:
                        quant_sig(i + 1, 0, 4)
                    stage1(i + 1)
                if step == "F" and i > GROUPS and g == 2:
                    for c in range(4):
                        finish(j - 1, c)
                if step == "V" and i in V_SQUARES:
                    square_on_vector(i)
                if step == "E" and i > 1:
                    quant_ratio(i - 2)
                    stage2(i - 2)
            if j in (1, 2) and g == 1:
                h_mix(j + 1, 0, "v")
                h_mix(j + 1, 1, "v")
            if j in (1, 2) and g == 2:
                h_quant(j + 1)
        quant_ratio(UNITS - 2)
        stage2(UNITS - 2)
        ratio(UNITS - 1)
        quant_ratio(UNITS - 1)
        stage2(UNITS - 1)
        for c in range(4):
            finish(3, c)
